import numpy as np, ml_dtypes
CORES = [1,129,9,137,57,185,105,233,113,241,121,249]
N = 12
F = 32
def setup_inputs(rng):
    return {"a": rng.standard_normal((N, 128, 128), dtype=np.float32).astype(ml_dtypes.bfloat16), "b": rng.standard_normal((N, 128, F), dtype=np.float32).astype(ml_dtypes.bfloat16)}
def setup_inputs_big(rng):
    d = setup_inputs(rng)
    for k in ("a", "b"): d[k] = (d[k].astype(np.float32) * 1024.0).astype(d[k].dtype)
    return d
def setup_inputs_small(rng):
    d = setup_inputs(rng)
    for k in ("a", "b"): d[k] = (d[k].astype(np.float32) * (1 / 1024.0)).astype(d[k].dtype)
    return d
def setup_inputs_apart(rng):
    d = setup_inputs(rng)
    f = (10.0 ** rng.permutation(np.linspace(-1.5, 1.5, N))).astype(np.float32).reshape(N, 1, 1)
    for k in ("a", "b"): d[k] = (d[k].astype(np.float32) * f).astype(d[k].dtype)
    return d
def reference(a, b):
    s = (a.astype(np.float64).sum(axis=0).T @ b.astype(np.float64).sum(axis=0)).astype(ml_dtypes.bfloat16 if a.dtype != np.float64 else np.float64)
    return {"y": np.broadcast_to(s, (N,) + s.shape)}

@@ -1,0 +1,154 @@
+from concourse.bass import DstId, RemoteDMATransfer
+
+N_CORES = 256
+ROWS, COLS, F = 128, 128, 32
+A_PIECES = ROWS * COLS // (128 * F)
+PIECES = A_PIECES + 1
+MAX_GROUP = 8
+KP = 64
+H = ROWS // KP
+
+SCRATCH = {
+    "pack": ("dram", [PIECES, 128, F], "bfloat16"),
+    "recv": ("dram", [MAX_GROUP, 128, F], "bfloat16"),
+    "land": ("dram", [2 * PIECES, 128, F], "bfloat16"),
+    "sa": ("sbuf", [128, 2 * H * COLS], "bfloat16"),
+    "sb": ("sbuf", [128, 2 * H * F], "bfloat16"),
+    "ps": ("psum", [128, F], "float32"),
+    "ys": ("sbuf", [128, F], "bfloat16"),
+}
+SEMAPHORES = ["ld", "sent", "rcv", "arr0", "arr1", "in0", "in1", "mm", "cp", "st"]
+
+_PLAN = {}
+
+
+def _engines(mask):
+    out = []
+    while mask:
+        low = mask & -mask
+        out.append(low)
+        mask ^= low
+    return out
+
+
+def _common_mask(topo, src, dsts):
+    m = topo.mask(src, dsts[0])
+    for d in dsts[1:]:
+        m &= topo.mask(src, d)
+    return m
+
+
+def _plan(ranks, topo):
+    if "p" in _PLAN:
+        return _PLAN["p"]
+    groups = []
+    for r in ranks:
+        for grp in groups:
+            if topo.same_plane(r, grp[0]):
+                grp.append(r)
+                break
+        else:
+            groups.append([r])
+    chips = {}
+    for c in range(N_CORES):
+        chips.setdefault((topo.host(c), topo.chip(c)), []).append(c)
+    busy = set((topo.host(r), topo.chip(r)) for r in ranks)
+    idle = [k for k in sorted(chips) if k not in busy]
+    pairs = []
+    for i, x in enumerate(idle):
+        for y in idle[i + 1:]:
+            if topo.mates(chips[x][0], chips[y][0]):
+                pairs.append(chips[x] + chips[y])
+    dies = sorted(set(topo.die(c) for c in range(N_CORES)))
+    table, slot = [], 0
+    for grp in groups:
+        row = []
+        for _q in range(PIECES):
+            pool = pairs[slot % len(pairs)]
+            d = dies[(slot + slot // len(pairs)) % len(dies)]
+            cand = [c for c in pool if topo.die(c) == d
+                    and all(topo.may_write(r, c) for r in grp)
+                    and all(topo.may_write(c, r) for r in ranks)]
+            row.append(cand[0])
+            slot += 1
+        table.append(row)
+    _PLAN["p"] = (groups, table)
+    return _PLAN["p"]
+
+
+def _summing_core(g, core, T, topo, ranks, grp, P, q):
+    eng = _engines(_common_mask(topo, core, ranks))
+    n = 1
+    while n * 2 <= len(eng):
+        n *= 2
+    mask = sum(eng[:n])
+    ids = []
+    for r in ranks:
+        rid, pid = topo.addr(r, core)
+        ids.append(DstId(rid=rid, pnc=pid))
+    g.wait_ge(T.sem.rcv, len(grp))
+    g.remote_dma_fused(
+        [RemoteDMATransfer(dst_ids=ids, dma_engine_mask=mask, remote_sem=T.sem["arr%d" % P],
+                           srcs=[T.recv[j] for j in range(len(grp))],
+                           dsts=[T.land[P * PIECES + q] for _r in ranks], alu_op=1)],
+        local_sem=T.sem.sent)
+    g.wait_ge(T.sem.sent, n)
+    return n
+
+
+def rank_program(g, core, T, topo):
+    ranks = list(T.cores)
+    groups, table = _plan(ranks, topo)
+    for P, row in enumerate(table):
+        for q, c in enumerate(row):
+            if c == core:
+                _summing_core(g, core, T, topo, ranks, groups[P], P, q)
+    if T.rank_of(core) is None:
+        return
+
+    mine = [P for P, grp in enumerate(groups) if core in grp][0]
+    j = groups[mine].index(core)
+
+    g.sync.dma_start(out=T.pack[0:A_PIECES], in_=T.a[:, :]).then_inc(T.sem.ld, 16)
+    g.scalar.dma_start(out=T.pack[A_PIECES], in_=T.b[:, :]).then_inc(T.sem.ld, 16)
+
+    eng = _engines(_common_mask(topo, core, table[mine]))
+    eng = eng[0::2] + eng[1::2]
+    transfers = []
+    for q, c in enumerate(table[mine]):
+        rid, pid = topo.addr(c, core)
+        transfers.append(RemoteDMATransfer(dst_ids=[DstId(rid=rid, pnc=pid)], dma_engine_mask=eng[q],
+                                           remote_sem=T.sem.rcv, src=T.pack[q], dst=T.recv[j]))
+    g.wait_ge(T.sem.ld, 32)
+    g.remote_dma_fused(transfers, local_sem=T.sem.sent)
+    g.wait_ge(T.sem.sent, PIECES)
+
+    for P in range(len(groups)):
+        n = 1
+        while n * 2 <= len(_engines(_common_mask(topo, table[P][0], ranks))):
+            n *= 2
+        arr, inn = T.sem["arr%d" % P], T.sem["in%d" % P]
+        g.sync.wait_ge(arr, PIECES * n)
+        g.sync.dma_start(out=T.sa[0:KP, P * H * COLS:(P + 1) * H * COLS],
+                         in_=T.land[P * PIECES:P * PIECES + A_PIECES]).then_inc(inn, 16)
+        g.scalar.wait_ge(arr, PIECES * n)
+        g.scalar.dma_start(out=T.sb[0:KP, P * H * F:(P + 1) * H * F],
+                           in_=T.land[P * PIECES + A_PIECES]).then_inc(inn, 16)
+
+    prods = [(0, 0, h) for h in range(H)]
+    prods += [(PA, PB, h) for (PA, PB) in ((0, 1), (1, 0), (1, 1)) for h in range(H)]
+    g.tensor.wait_ge(T.sem.in0, 32)
+    for i, (PA, PB, h) in enumerate(prods):
+        if i == H:
+            g.tensor.wait_ge(T.sem.in1, 32)
+        mm = g.tensor.matmul(T.ps[:, :],
+                             T.sa[0:KP, (PA * H + h) * COLS:(PA * H + h + 1) * COLS],
+                             T.sb[0:KP, (PB * H + h) * F:(PB * H + h + 1) * F],
+                             start=(i == 0), stop=(i == len(prods) - 1))
+    mm.then_inc(T.sem.mm, 1)
+
+    g.vector.wait_ge(T.sem.mm, 1)
+    g.vector.tensor_copy(out=T.ys[:, :], in_=T.ps[:, :]).then_inc(T.sem.cp, 1)
+    g.sync.wait_ge(T.sem.cp, 1)
+    g.sync.dma_start(out=T.y[:, :], in_=T.ys[:, :]).then_inc(T.sem.st, 16)
+    g.sync.wait_ge(T.sem.st, 16)

@@ -2,22 +2,24 @@ from concourse.bass import DstId, RemoteDMATransfer
 
 N_CORES = 256
 ROWS, COLS, F = 128, 128, 32
-A_PIECES = ROWS * COLS // (128 * F)
-PIECES = A_PIECES + 1
+W = 16
+A_PIECES = ROWS * COLS // (128 * W)
+B_PIECES = ROWS * F // (128 * W)
+PIECES = A_PIECES + B_PIECES
 MAX_GROUP = 8
 KP = 64
 H = ROWS // KP
 
 SCRATCH = {
-    "pack": ("dram", [PIECES, 128, F], "bfloat16"),
-    "recv": ("dram", [MAX_GROUP, 128, F], "bfloat16"),
-    "land": ("dram", [2 * PIECES, 128, F], "bfloat16"),
+    "pack": ("dram", [PIECES, 128, W], "bfloat16"),
+    "recv": ("dram", [MAX_GROUP, 128, W], "bfloat16"),
+    "land": ("dram", [2 * PIECES, 128, W], "bfloat16"),
     "sa": ("sbuf", [128, 2 * H * COLS], "bfloat16"),
     "sb": ("sbuf", [128, 2 * H * F], "bfloat16"),
     "ps": ("psum", [128, F], "float32"),
     "ys": ("sbuf", [128, F], "bfloat16"),
 }
-SEMAPHORES = ["ld", "sent", "rcv", "arr0", "arr1", "in0", "in1", "mm", "cp", "st"]
+SEMAPHORES = ["lda", "ldb", "sent", "rcv", "arrA0", "arrA1", "arrB0", "arrB1", "in0", "in1", "mm", "cp", "st"]
 
 _PLAN = {}
 
@@ -31,11 +33,19 @@ def _engines(mask):
     return out
 
 
-def _common_mask(topo, src, dsts):
+def _pow2(n):
+    p = 1
+    while p * 2 <= n:
+        p *= 2
+    return p
+
+
+def _common_engines(topo, src, dsts):
     m = topo.mask(src, dsts[0])
     for d in dsts[1:]:
         m &= topo.mask(src, d)
-    return m
+    eng = _engines(m)
+    return eng[:_pow2(len(eng))]
 
 
 def _plan(ranks, topo):
@@ -53,47 +63,52 @@ def _plan(ranks, topo):
     for c in range(N_CORES):
         chips.setdefault((topo.host(c), topo.chip(c)), []).append(c)
     busy = set((topo.host(r), topo.chip(r)) for r in ranks)
-    idle = [k for k in sorted(chips) if k not in busy]
-    pairs = []
-    for i, x in enumerate(idle):
-        for y in idle[i + 1:]:
+    keys = sorted(chips)
+    found = []
+    for i, x in enumerate(keys):
+        for y in keys[i + 1:]:
             if topo.mates(chips[x][0], chips[y][0]):
-                pairs.append(chips[x] + chips[y])
+                found.append((len(busy & set((x, y))), chips[x] + chips[y]))
+    pairs = [p for n, p in found if n == 0] + [p for n, p in found if n == 1]
     dies = sorted(set(topo.die(c) for c in range(N_CORES)))
-    table, slot = [], 0
-    for grp in groups:
+    largest = max(len(grp) for grp in groups)
+    table = []
+    for P, grp in enumerate(groups):
         row = []
-        for _q in range(PIECES):
-            pool = pairs[slot % len(pairs)]
-            d = dies[(slot + slot // len(pairs)) % len(dies)]
-            cand = [c for c in pool if topo.die(c) == d
+        for q in range(PIECES):
+            p = q if len(grp) == largest else len(pairs) - 1 - q
+            d = dies[(p + P) % len(dies)]
+            cand = [c for c in pairs[p] if topo.die(c) == d and c not in ranks
                     and all(topo.may_write(r, c) for r in grp)
                     and all(topo.may_write(c, r) for r in ranks)]
             row.append(cand[0])
-            slot += 1
         table.append(row)
     _PLAN["p"] = (groups, table)
     return _PLAN["p"]
 
 
-def _summing_core(g, core, T, topo, ranks, grp, P, q):
-    eng = _engines(_common_mask(topo, core, ranks))
-    n = 1
-    while n * 2 <= len(eng):
-        n *= 2
-    mask = sum(eng[:n])
+def _scatter_masks(topo, core, row):
+    eng = _common_engines(topo, core, row)
+    per = _pow2(len(eng) // B_PIECES)
+    return [[eng[q]] for q in range(A_PIECES)] + [eng[i * per:(i + 1) * per] for i in range(B_PIECES)]
+
+
+def _summing_core(g, core, T, topo, ranks, grp, row, P, q):
+    eng = _common_engines(topo, core, ranks)
+    first = (q + P) % len(ranks)
+    order = ranks[first:] + ranks[:first]
     ids = []
-    for r in ranks:
+    for r in order:
         rid, pid = topo.addr(r, core)
         ids.append(DstId(rid=rid, pnc=pid))
-    g.wait_ge(T.sem.rcv, len(grp))
+    arr = T.sem["arr%s%d" % ("A" if q < A_PIECES else "B", P)]
+    g.wait_ge(T.sem.rcv, sum(len(_scatter_masks(topo, r, row)[q]) for r in grp))
     g.remote_dma_fused(
-        [RemoteDMATransfer(dst_ids=ids, dma_engine_mask=mask, remote_sem=T.sem["arr%d" % P],
+        [RemoteDMATransfer(dst_ids=ids, dma_engine_mask=sum(eng), remote_sem=arr,
                            srcs=[T.recv[j] for j in range(len(grp))],
-                           dsts=[T.land[P * PIECES + q] for _r in ranks], alu_op=1)],
+                           dsts=[T.land[P * PIECES + q] for _r in order], alu_op=1)],
         local_sem=T.sem.sent)
-    g.wait_ge(T.sem.sent, n)
-    return n
+    g.wait_ge(T.sem.sent, len(eng))
 
 
 def rank_program(g, core, T, topo):
@@ -102,38 +117,37 @@ def rank_program(g, core, T, topo):
     for P, row in enumerate(table):
         for q, c in enumerate(row):
             if c == core:
-                _summing_core(g, core, T, topo, ranks, groups[P], P, q)
+                _summing_core(g, core, T, topo, ranks, groups[P], row, P, q)
     if T.rank_of(core) is None:
         return
 
     mine = [P for P, grp in enumerate(groups) if core in grp][0]
     j = groups[mine].index(core)
 
-    g.sync.dma_start(out=T.pack[0:A_PIECES], in_=T.a[:, :]).then_inc(T.sem.ld, 16)
-    g.scalar.dma_start(out=T.pack[A_PIECES], in_=T.b[:, :]).then_inc(T.sem.ld, 16)
+    g.sync.dma_start(out=T.pack[0:A_PIECES], in_=T.a[:, :]).then_inc(T.sem.lda, 16)
+    g.scalar.dma_start(out=T.pack[A_PIECES:PIECES], in_=T.b[:, :]).then_inc(T.sem.ldb, 16)
 
-    eng = _engines(_common_mask(topo, core, table[mine]))
-    eng = eng[0::2] + eng[1::2]
+    masks = _scatter_masks(topo, core, table[mine])
     transfers = []
     for q, c in enumerate(table[mine]):
         rid, pid = topo.addr(c, core)
-        transfers.append(RemoteDMATransfer(dst_ids=[DstId(rid=rid, pnc=pid)], dma_engine_mask=eng[q],
+        transfers.append(RemoteDMATransfer(dst_ids=[DstId(rid=rid, pnc=pid)], dma_engine_mask=sum(masks[q]),
                                            remote_sem=T.sem.rcv, src=T.pack[q], dst=T.recv[j]))
-    g.wait_ge(T.sem.ld, 32)
-    g.remote_dma_fused(transfers, local_sem=T.sem.sent)
-    g.wait_ge(T.sem.sent, PIECES)
+    g.wait_ge(T.sem.lda, 16)
+    g.remote_dma_fused(transfers[:A_PIECES], local_sem=T.sem.sent)
+    g.wait_ge(T.sem.ldb, 16)
+    g.remote_dma_fused(transfers[A_PIECES:], local_sem=T.sem.sent)
+    g.wait_ge(T.sem.sent, sum(len(m) for m in masks))
 
     for P in range(len(groups)):
-        n = 1
-        while n * 2 <= len(_engines(_common_mask(topo, table[P][0], ranks))):
-            n *= 2
-        arr, inn = T.sem["arr%d" % P], T.sem["in%d" % P]
-        g.sync.wait_ge(arr, PIECES * n)
+        incs = [len(_common_engines(topo, c, ranks)) for c in table[P]]
+        inn = T.sem["in%d" % P]
+        g.sync.wait_ge(T.sem["arrA%d" % P], sum(incs[:A_PIECES]))
         g.sync.dma_start(out=T.sa[0:KP, P * H * COLS:(P + 1) * H * COLS],
                          in_=T.land[P * PIECES:P * PIECES + A_PIECES]).then_inc(inn, 16)
-        g.scalar.wait_ge(arr, PIECES * n)
+        g.scalar.wait_ge(T.sem["arrB%d" % P], sum(incs[A_PIECES:]))
         g.scalar.dma_start(out=T.sb[0:KP, P * H * F:(P + 1) * H * F],
-                           in_=T.land[P * PIECES + A_PIECES]).then_inc(inn, 16)
+                           in_=T.land[P * PIECES + A_PIECES:(P + 1) * PIECES]).then_inc(inn, 16)
 
     prods = [(0, 0, h) for h in range(H)]
     prods += [(PA, PB, h) for (PA, PB) in ((0, 1), (1, 0), (1, 1)) for h in range(H)]

from concourse.bass import DstId, RemoteDMATransfer

N_CORES = 256
ROWS, COLS, F = 128, 128, 32
W = 16
A_PIECES = ROWS * COLS // (128 * W)
B_PIECES = ROWS * F // (128 * W)
PIECES = A_PIECES + B_PIECES
MAX_GROUP = 8
KP = 64
H = ROWS // KP

SCRATCH = {
    "pack": ("dram", [PIECES, 128, W], "bfloat16"),
    "recv": ("dram", [MAX_GROUP, 128, W], "bfloat16"),
    "land": ("dram", [2 * PIECES, 128, W], "bfloat16"),
    "sa": ("sbuf", [128, 2 * H * COLS], "bfloat16"),
    "sb": ("sbuf", [128, 2 * H * F], "bfloat16"),
    "ps": ("psum", [128, F], "float32"),
    "ys": ("sbuf", [128, F], "bfloat16"),
}
SEMAPHORES = ["lda", "ldb", "sent", "rcv", "arrA0", "arrA1", "arrB0", "arrB1", "in0", "in1", "mm", "cp", "st"]

_PLAN = {}


def _engines(mask):
    out = []
    while mask:
        low = mask & -mask
        out.append(low)
        mask ^= low
    return out


def _pow2(n):
    p = 1
    while p * 2 <= n:
        p *= 2
    return p


def _common_engines(topo, src, dsts):
    m = topo.mask(src, dsts[0])
    for d in dsts[1:]:
        m &= topo.mask(src, d)
    eng = _engines(m)
    return eng[:_pow2(len(eng))]


def _plan(ranks, topo):
    if "p" in _PLAN:
        return _PLAN["p"]
    groups = []
    for r in ranks:
        for grp in groups:
            if topo.same_plane(r, grp[0]):
                grp.append(r)
                break
        else:
            groups.append([r])
    chips = {}
    for c in range(N_CORES):
        chips.setdefault((topo.host(c), topo.chip(c)), []).append(c)
    busy = set((topo.host(r), topo.chip(r)) for r in ranks)
    keys = sorted(chips)
    found = []
    for i, x in enumerate(keys):
        for y in keys[i + 1:]:
            if topo.mates(chips[x][0], chips[y][0]):
                found.append((len(busy & set((x, y))), chips[x] + chips[y]))
    pairs = [p for n, p in found if n == 0] + [p for n, p in found if n == 1]
    dies = sorted(set(topo.die(c) for c in range(N_CORES)))
    largest = max(len(grp) for grp in groups)
    table = []
    for P, grp in enumerate(groups):
        row = []
        for q in range(PIECES):
            p = q if len(grp) == largest else len(pairs) - 1 - q
            d = dies[(p + P) % len(dies)]
            cand = [c for c in pairs[p] if topo.die(c) == d and c not in ranks
                    and all(topo.may_write(r, c) for r in grp)
                    and all(topo.may_write(c, r) for r in ranks)]
            row.append(cand[0])
        table.append(row)
    _PLAN["p"] = (groups, table)
    return _PLAN["p"]


def _scatter_masks(topo, core, row):
    eng = _common_engines(topo, core, row)
    per = _pow2(len(eng) // B_PIECES)
    return [[eng[q]] for q in range(A_PIECES)] + [eng[i * per:(i + 1) * per] for i in range(B_PIECES)]


def _summing_core(g, core, T, topo, ranks, grp, row, P, q):
    eng = _common_engines(topo, core, ranks)
    first = (q + P) % len(ranks)
    order = ranks[first:] + ranks[:first]
    ids = []
    for r in order:
        rid, pid = topo.addr(r, core)
        ids.append(DstId(rid=rid, pnc=pid))
    arr = T.sem["arr%s%d" % ("A" if q < A_PIECES else "B", P)]
    g.wait_ge(T.sem.rcv, sum(len(_scatter_masks(topo, r, row)[q]) for r in grp))
    g.remote_dma_fused(
        [RemoteDMATransfer(dst_ids=ids, dma_engine_mask=sum(eng), remote_sem=arr,
                           srcs=[T.recv[j] for j in range(len(grp))],
                           dsts=[T.land[P * PIECES + q] for _r in order], alu_op=1)],
        local_sem=T.sem.sent)
    g.wait_ge(T.sem.sent, len(eng))


def rank_program(g, core, T, topo):
    ranks = list(T.cores)
    groups, table = _plan(ranks, topo)
    for P, row in enumerate(table):
        for q, c in enumerate(row):
            if c == core:
                _summing_core(g, core, T, topo, ranks, groups[P], row, P, q)
    if T.rank_of(core) is None:
        return

    mine = [P for P, grp in enumerate(groups) if core in grp][0]
    j = groups[mine].index(core)

    g.sync.dma_start(out=T.pack[0:A_PIECES], in_=T.a[:, :]).then_inc(T.sem.lda, 16)
    g.scalar.dma_start(out=T.pack[A_PIECES:PIECES], in_=T.b[:, :]).then_inc(T.sem.ldb, 16)

    masks = _scatter_masks(topo, core, table[mine])
    transfers = []
    for q, c in enumerate(table[mine]):
        rid, pid = topo.addr(c, core)
        transfers.append(RemoteDMATransfer(dst_ids=[DstId(rid=rid, pnc=pid)], dma_engine_mask=sum(masks[q]),
                                           remote_sem=T.sem.rcv, src=T.pack[q], dst=T.recv[j]))
    g.wait_ge(T.sem.lda, 16)
    g.remote_dma_fused(transfers[:A_PIECES], local_sem=T.sem.sent)
    g.wait_ge(T.sem.ldb, 16)
    g.remote_dma_fused(transfers[A_PIECES:], local_sem=T.sem.sent)
    g.wait_ge(T.sem.sent, sum(len(m) for m in masks))

    for P in range(len(groups)):
        incs = [len(_common_engines(topo, c, ranks)) for c in table[P]]
        inn = T.sem["in%d" % P]
        g.sync.wait_ge(T.sem["arrA%d" % P], sum(incs[:A_PIECES]))
        g.sync.dma_start(out=T.sa[0:KP, P * H * COLS:(P + 1) * H * COLS],
                         in_=T.land[P * PIECES:P * PIECES + A_PIECES]).then_inc(inn, 16)
        g.scalar.wait_ge(T.sem["arrB%d" % P], sum(incs[A_PIECES:]))
        g.scalar.dma_start(out=T.sb[0:KP, P * H * F:(P + 1) * H * F],
                           in_=T.land[P * PIECES + A_PIECES:(P + 1) * PIECES]).then_inc(inn, 16)

    prods = [(0, 0, h) for h in range(H)]
    prods += [(PA, PB, h) for (PA, PB) in ((0, 1), (1, 0), (1, 1)) for h in range(H)]
    g.tensor.wait_ge(T.sem.in0, 32)
    for i, (PA, PB, h) in enumerate(prods):
        if i == H:
            g.tensor.wait_ge(T.sem.in1, 32)
        mm = g.tensor.matmul(T.ps[:, :],
                             T.sa[0:KP, (PA * H + h) * COLS:(PA * H + h + 1) * COLS],
                             T.sb[0:KP, (PB * H + h) * F:(PB * H + h + 1) * F],
                             start=(i == 0), stop=(i == len(prods) - 1))
    mm.then_inc(T.sem.mm, 1)

    g.vector.wait_ge(T.sem.mm, 1)
    g.vector.tensor_copy(out=T.ys[:, :], in_=T.ps[:, :]).then_inc(T.sem.cp, 1)
    g.sync.wait_ge(T.sem.cp, 1)
    g.sync.dma_start(out=T.y[:, :], in_=T.ys[:, :]).then_inc(T.sem.st, 16)
    g.sync.wait_ge(T.sem.st, 16)
